import numpy as np
import ml_dtypes


def mxq(x, axis, fmt="e4m3"):
    dtype, down = {"e4m3": (ml_dtypes.float8_e4m3fn, 7), "e5m2": (ml_dtypes.float8_e5m2, 14)}[fmt]
    v = np.moveaxis(np.asarray(x, np.float32).astype(ml_dtypes.bfloat16).astype(np.float64), axis, -1)
    blocks = v.reshape(v.shape[:-1] + (-1, 32))
    amax = np.abs(blocks).max(-1, keepdims=True)
    byte = np.maximum(np.where(amax > 0, np.frexp(amax)[1] - 1 + 127, 0) - down, 1)
    scale = np.exp2(byte - 127.0)
    codes = (blocks / scale).astype(np.float32).astype(dtype).astype(np.float64)
    return np.moveaxis((codes * scale).reshape(v.shape), -1, axis)


WIDE = False


def mx_kscale(k):
    if not WIDE:
        return np.ones(k)
    levels = np.array([10, -10, 5, -5, 0])
    if k % 512:
        return np.exp2(np.random.permutation(np.resize(levels, k // 32))).repeat(32)
    a = np.empty((k // 512, 16))
    for p in range(k // 512):
        a[p, :8] = np.random.permutation(np.resize(levels, 8))
        for g in range(8):
            far = levels[np.abs(levels - a[p, g]) >= 10]
            a[p, g + 8] = far[np.random.randint(len(far))]
    return np.exp2(a.ravel()).repeat(32)


def f64(x):
    return np.asarray(x).astype(np.float64)


def striped8(idx):
    return np.asarray(idx).reshape(8, -1, 16).transpose(0, 2, 1).reshape(128, -1).astype(np.uint16)


def unstriped8(offs):
    return offs.reshape(8, 16, -1).transpose(0, 2, 1).reshape(8, -1).astype(np.int64)


def pick8(x, idx, run):
    r = np.arange(len(x))
    return x[r[:, None], idx[r % (8 * run) // run]]


E2M1 = np.array([0.0, 0.5, 1.0, 1.5, 2.0, 3.0, 4.0, 6.0, -0.0, -0.5, -1.0, -1.5, -2.0, -3.0, -4.0, -6.0])


def pack_weight(w, fmt):
    k, n = w.shape
    w = f64(np.asarray(w, np.float32).astype(ml_dtypes.bfloat16)).reshape(k // 32, 32, n)
    amax = np.abs(w).max(1)
    if fmt == "e4m3":
        byte = np.frexp(amax)[1] - 1 + 127 - 7
    else:
        mant, ex = np.frexp(amax / 6.0)
        byte = np.where(mant > 0.5, ex, ex - 1) + 127
    byte = np.clip(np.where(amax > 0, byte, 1), 1, 254)
    scaled = (w * np.exp2(127.0 - byte)[:, None, :]).reshape(k, n).astype(np.float32)
    by_word = np.ascontiguousarray(scaled.reshape(k // 512, 128, 4, n).transpose(0, 1, 3, 2))
    if fmt == "e4m3":
        words = by_word.astype(ml_dtypes.float8_e4m3fn).view(np.uint8)
    else:
        c = by_word.astype(ml_dtypes.float4_e2m1fn).view(np.uint8) & 0xF
        words = (c[..., 0::2] | (c[..., 1::2] << 4)).reshape(k // 512, 128, 2 * n)
    return np.ascontiguousarray(words), np.ascontiguousarray(byte.astype(np.uint8).reshape(k // 512, 16, n))


def unpack_weight(words, scales, fmt):
    g, _, n = scales.shape
    words = np.ascontiguousarray(words).reshape(g, 128, n, -1)
    if fmt == "e4m3":
        vals = words.view(ml_dtypes.float8_e4m3fn).astype(np.float64)
    else:
        nib = np.empty((g, 128, n, 4), np.uint8)
        nib[..., 0::2] = words & 0xF
        nib[..., 1::2] = words >> 4
        vals = E2M1[nib]
    vals = vals * np.repeat(np.exp2(scales.astype(np.float64) - 127.0), 8, axis=1)[..., None]
    return vals.transpose(0, 1, 3, 2).reshape(g * 512, n)


D, T, U, I, Q = 512, 1024, 1024, 512, 128


def setup_inputs():
    n = np.random.standard_normal
    idx = np.stack([np.random.permutation(T)[:I] for _ in range(8)])
    idx2 = np.stack([np.random.permutation(U)[:I] for _ in range(8)])
    idx3 = np.stack([np.random.permutation(T)[:I] for _ in range(8)])
    idx4 = np.stack([np.random.permutation(U)[:I] for _ in range(8)])
    idx5 = np.stack([np.random.permutation(T)[:I] for _ in range(8)])
    idx6 = np.stack([np.random.permutation(T)[:I] for _ in range(8)])
    fd = mx_kscale(D)
    keysp = pack_weight(n((D, T)) / fd[:, None], "e2m1")
    notesp = pack_weight(n((D, U)) / fd[:, None], "e4m3")
    return {
        "query": (n((D, Q)) * 1.0 / np.sqrt(D) * fd[:, None]).astype(np.float32),
        "keys_words": keysp[0],
        "keys_scales": keysp[1],
        "notes_words": notesp[0],
        "notes_scales": notesp[1],
        "offs": striped8(idx),
        "offs2": striped8(idx2),
        "offs3": striped8(idx3),
        "offs4": striped8(idx4),
        "offs5": striped8(idx5),
        "offs6": striped8(idx6),
    }


def reference(query, keys_words, keys_scales, notes_words, notes_scales, offs, offs2, offs3, offs4, offs5, offs6):
    idx = unstriped8(offs)
    idx2 = unstriped8(offs2)
    idx3 = unstriped8(offs3)
    idx4 = unstriped8(offs4)
    idx5 = unstriped8(offs5)
    idx6 = unstriped8(offs6)
    keysu = unpack_weight(keys_words, keys_scales, "e2m1")
    notesu = unpack_weight(notes_words, notes_scales, "e4m3")
    queryq = mxq(f64(query), 0, "e4m3")
    a = queryq.T @ keysu
    b = queryq.T @ notesu
    w = np.maximum(pick8(a, idx, 16), pick8(b, idx2, 16))
    v = np.maximum(pick8(a, idx3, 16), pick8(b, idx4, 16))
    r = w - v
    f1 = np.zeros((Q, T))
    f1[np.arange(Q)[:, None], idx5[np.arange(Q) % 128 // 16]] = r
    cc = a - f1
    y = pick8(cc, idx6, 16)
    return y

@@ -1,0 +1,119 @@
+from contextlib import ExitStack
+
+import concourse.mybir as mybir
+
+D, T, U, SLOTS, Q = 512, 1024, 1024, 512, 128
+FLOPS = 2 * D * Q * (T + U)
+
+F32 = mybir.dt.float32
+BF16 = mybir.dt.bfloat16
+I32 = mybir.dt.int32
+U32 = mybir.dt.uint32
+U16 = mybir.dt.uint16
+U8 = mybir.dt.uint8
+FP8X4 = mybir.dt.float8_e4m3fn_x4
+FP4X4 = mybir.dt.float4_e2m1fn_x4
+ALU = mybir.AluOpType
+COPY = mybir.ActivationFunctionType.Copy
+
+P = 128
+PACK = 4
+N_PASS = 256
+HALF = SLOTS // 2
+HALF_COLS = HALF // 16
+
+
+def tile_attend_teams_two_kernel(tc, query, keys_words, keys_scales, notes_words, notes_scales,
+                                  offs, offs2, offs3, offs4, offs5, offs6, out):
+    nc = tc.nc
+    with ExitStack() as ctx:
+        sb = ctx.enter_context(tc.tile_pool(name="sb", bufs=1))
+        ps = ctx.enter_context(tc.psum_pool(name="ps", bufs=1))
+
+        q_raw = sb.tile([P, PACK, Q], F32, align_bytes=64)
+        q_bf = sb.tile([P, Q, PACK], BF16, align_bytes=64)
+        q_codes = sb.tile([P, Q], U32, align_bytes=64)
+        q_scales = sb.tile([P, Q], U8, align_bytes=64)
+        k_words = sb.tile([P, 2 * T], U8, align_bytes=64)
+        k_scales = sb.tile([P, T], U8, align_bytes=64)
+        n_words = sb.tile([P, U], U32, align_bytes=64)
+        n_scales = sb.tile([P, U], U8, align_bytes=64)
+        a = sb.tile([P, T], F32, align_bytes=64)
+        b = sb.tile([P, U], F32, align_bytes=64)
+        f1 = sb.tile([P, T], F32, align_bytes=64)
+        cc = sb.tile([P, T], F32, align_bytes=64)
+        lists = [sb.tile([P, SLOTS // 16], U16, name="list%d" % j) for j in range(6)]
+
+        nc.scalar.dma_start(q_raw[:], query.rearrange("(p j) q -> p j q", j=PACK))
+        nc.vector.memset(k_scales[:].bitcast(I32), 0)
+        nc.vector.memset(n_scales[:].bitcast(I32), 0)
+        for g in range(4):
+            nc.sync.dma_start(k_scales[32 * g:32 * g + 4, :].bitcast(I32),
+                              keys_scales[0, 4 * g:4 * g + 4, :].bitcast(I32))
+        nc.sync.dma_start(k_words[:].bitcast(I32), keys_words[0].bitcast(I32))
+        nc.sync.dma_start(n_words[:].bitcast(I32),
+                          notes_words[0].rearrange("p n t -> p (n t)").bitcast(I32))
+        for g in range(4):
+            nc.sync.dma_start(n_scales[32 * g:32 * g + 4, :].bitcast(I32),
+                              notes_scales[0, 4 * g:4 * g + 4, :].bitcast(I32))
+        sources = [offs, offs2, offs3, offs4, offs5, offs6]
+        for j in (0, 2, 1, 3, 4, 5):
+            nc.sync.dma_start(lists[j][:], sources[j])
+        nc.vector.memset(f1[:], 0.0)
+
+        nc.vector.tensor_copy(q_bf[:], q_raw[:].rearrange("p j q -> p q j"))
+        nc.vector.quantize_mx(out=q_codes[:].bitcast(FP8X4), scales=q_scales[:],
+                              in_=q_bf[:].rearrange("p q j -> p (q j)"))
+
+        def scores(name, c, words, scales):
+            bank = ps.tile([P, N_PASS], F32, name=name)
+            nc.tensor.matmul_mx(out=bank[:], lhsT=q_codes[:].bitcast(FP8X4), lhsT_scale=q_scales[:],
+                                rhs=words, rhs_scale=scales[:, c * N_PASS:(c + 1) * N_PASS],
+                                start=True, stop=True)
+            return bank
+
+        for c in range(T // N_PASS):
+            cols = slice(c * N_PASS, (c + 1) * N_PASS)
+            bank = scores("a%d" % c, c, k_words[:, 2 * c * N_PASS:2 * (c + 1) * N_PASS].bitcast(FP4X4), k_scales)
+            if c % 2 == 0:
+                nc.scalar.activation(a[:, cols], bank[:], COPY)
+            else:
+                nc.vector.tensor_copy(a[:, cols], bank[:])
+        for c in range(U // N_PASS):
+            cols = slice(c * N_PASS, (c + 1) * N_PASS)
+            bank = scores("b%d" % c, c, n_words[:, cols].bitcast(FP8X4), n_scales)
+            nc.scalar.activation(b[:, cols], bank[:], COPY)
+
+        def picked(window, j, h):
+            return window[:].indirect(lists[j][:, h * HALF_COLS:(h + 1) * HALF_COLS])
+
+        for h in range(2):
+            tok1 = sb.tile([P, HALF], F32, name="tok1")
+            note1 = sb.tile([P, HALF], F32, name="note1_%d" % h)
+            tok2 = sb.tile([P, HALF], F32, name="tok2")
+            neg_note2 = sb.tile([P, HALF], F32, name="neg_note2_%d" % h)
+            w = sb.tile([P, HALF], F32, name="w")
+            neg_v = sb.tile([P, HALF], F32, name="neg_v")
+            if h == 0:
+                nc.vector.tensor_copy(tok1[:], picked(a, 0, h))
+                nc.vector.tensor_copy(tok2[:], picked(a, 2, h))
+                nc.scalar.activation(neg_note2[:], picked(b, 3, h), COPY, scale=-1.0)
+                nc.vector.tensor_copy(note1[:], picked(b, 1, h))
+                nc.vector.scalar_tensor_tensor(neg_v[:], tok2[:], -1.0, neg_note2[:], ALU.mult, ALU.min)
+                nc.vector.tensor_tensor(w[:], tok1[:], note1[:], ALU.max)
+            else:
+                nc.scalar.activation(neg_note2[:], picked(b, 3, h), COPY, scale=-1.0)
+                nc.scalar.activation(note1[:], picked(b, 1, h), COPY)
+                nc.scalar.activation(tok2[:], picked(a, 2, h), COPY)
+                nc.scalar.activation(tok1[:], picked(a, 0, h), COPY)
+                nc.vector.scalar_tensor_tensor(neg_v[:], tok2[:], -1.0, neg_note2[:], ALU.mult, ALU.min)
+                nc.vector.tensor_tensor(w[:], tok1[:], note1[:], ALU.max)
+            nc.vector.tensor_tensor(picked(f1, 4, h), w[:], neg_v[:], ALU.add)
+
+        nc.vector.tensor_tensor(cc[:], a[:], f1[:], ALU.subtract)
+        y0 = sb.tile([P, HALF], F32)
+        y1 = sb.tile([P, HALF], F32)
+        nc.vector.tensor_copy(y0[:], picked(cc, 5, 0))
+        nc.scalar.activation(y1[:], picked(cc, 5, 1), COPY)
+        nc.sync.dma_start(out[:, 0:HALF], y0[:])
+        nc.scalar.dma_start(out[:, HALF:SLOTS], y1[:])

@@ -44,7 +44,7 @@ def tile_attend_teams_two_kernel(tc, query, keys_words, keys_scales, notes_words
         cc = sb.tile([P, T], F32, align_bytes=64)
         lists = [sb.tile([P, SLOTS // 16], U16, name="list%d" % j) for j in range(6)]
 
-        nc.scalar.dma_start(q_raw[:], query.rearrange("(p j) q -> p j q", j=PACK))
+        nc.sync.dma_start(q_raw[:], query.rearrange("(p j) q -> p j q", j=PACK))
         nc.vector.memset(k_scales[:].bitcast(I32), 0)
         nc.vector.memset(n_scales[:].bitcast(I32), 0)
         for g in range(4):
@@ -61,9 +61,13 @@ def tile_attend_teams_two_kernel(tc, query, keys_words, keys_scales, notes_words
             nc.sync.dma_start(lists[j][:], sources[j])
         nc.vector.memset(f1[:], 0.0)
 
-        nc.vector.tensor_copy(q_bf[:], q_raw[:].rearrange("p j q -> p q j"))
-        nc.vector.quantize_mx(out=q_codes[:].bitcast(FP8X4), scales=q_scales[:],
-                              in_=q_bf[:].rearrange("p q j -> p (q j)"))
+        for u in range(2):
+            rows = slice(u * Q // 2, (u + 1) * Q // 2)
+            nc.vector.tensor_copy(q_bf[:, rows, :], q_raw[:, :, rows].rearrange("p j q -> p q j"))
+        for u in range(2):
+            rows = slice(u * Q // 2, (u + 1) * Q // 2)
+            nc.vector.quantize_mx(out=q_codes[:, rows].bitcast(FP8X4), scales=q_scales[:, rows],
+                                  in_=q_bf[:, rows, :].rearrange("p q j -> p (q j)"))
 
         def scores(name, c, words, scales):
             bank = ps.tile([P, N_PASS], F32, name=name)

@@ -76,9 +76,11 @@ def tile_attend_teams_two_kernel(tc, query, keys_words, keys_scales, notes_words
                                 start=True, stop=True)
             return bank
 
+        a_banks = []
         for c in range(T // N_PASS):
             cols = slice(c * N_PASS, (c + 1) * N_PASS)
             bank = scores("a%d" % c, c, k_words[:, 2 * c * N_PASS:2 * (c + 1) * N_PASS].bitcast(FP4X4), k_scales)
+            a_banks.append(bank)
             if c % 2 == 0:
                 nc.scalar.activation(a[:, cols], bank[:], COPY)
             else:
@@ -114,7 +116,11 @@ def tile_attend_teams_two_kernel(tc, query, keys_words, keys_scales, notes_words
                 nc.vector.tensor_tensor(w[:], tok1[:], note1[:], ALU.max)
             nc.vector.tensor_tensor(picked(f1, 4, h), w[:], neg_v[:], ALU.add)
 
-        nc.vector.tensor_tensor(cc[:], a[:], f1[:], ALU.subtract)
+        last = slice(T - N_PASS, T)
+        nc.gpsimd.tensor_tensor(cc[:, last], a[:, last], f1[:, last], ALU.subtract)
+        for c in range(T // N_PASS - 1):
+            cols = slice(c * N_PASS, (c + 1) * N_PASS)
+            nc.vector.tensor_tensor(cc[:, cols], a_banks[c][:], f1[:, cols], ALU.subtract)
         y0 = sb.tile([P, HALF], F32)
         y1 = sb.tile([P, HALF], F32)
         nc.vector.tensor_copy(y0[:], picked(cc, 5, 0))

from contextlib import ExitStack

import concourse.mybir as mybir

D, T, U, SLOTS, Q = 512, 1024, 1024, 512, 128
FLOPS = 2 * D * Q * (T + U)

F32 = mybir.dt.float32
BF16 = mybir.dt.bfloat16
I32 = mybir.dt.int32
U32 = mybir.dt.uint32
U16 = mybir.dt.uint16
U8 = mybir.dt.uint8
FP8X4 = mybir.dt.float8_e4m3fn_x4
FP4X4 = mybir.dt.float4_e2m1fn_x4
ALU = mybir.AluOpType
COPY = mybir.ActivationFunctionType.Copy

P = 128
PACK = 4
N_PASS = 256
HALF = SLOTS // 2
HALF_COLS = HALF // 16


def tile_attend_teams_two_kernel(tc, query, keys_words, keys_scales, notes_words, notes_scales,
                                  offs, offs2, offs3, offs4, offs5, offs6, out):
    nc = tc.nc
    with ExitStack() as ctx:
        sb = ctx.enter_context(tc.tile_pool(name="sb", bufs=1))
        ps = ctx.enter_context(tc.psum_pool(name="ps", bufs=1))

        q_raw = sb.tile([P, PACK, Q], F32, align_bytes=64)
        q_bf = sb.tile([P, Q, PACK], BF16, align_bytes=64)
        q_codes = sb.tile([P, Q], U32, align_bytes=64)
        q_scales = sb.tile([P, Q], U8, align_bytes=64)
        k_words = sb.tile([P, 2 * T], U8, align_bytes=64)
        k_scales = sb.tile([P, T], U8, align_bytes=64)
        n_words = sb.tile([P, U], U32, align_bytes=64)
        n_scales = sb.tile([P, U], U8, align_bytes=64)
        a = sb.tile([P, T], F32, align_bytes=64)
        b = sb.tile([P, U], F32, align_bytes=64)
        f1 = sb.tile([P, T], F32, align_bytes=64)
        cc = sb.tile([P, T], F32, align_bytes=64)
        lists = [sb.tile([P, SLOTS // 16], U16, name="list%d" % j) for j in range(6)]

        nc.sync.dma_start(q_raw[:], query.rearrange("(p j) q -> p j q", j=PACK))
        nc.vector.memset(k_scales[:].bitcast(I32), 0)
        nc.vector.memset(n_scales[:].bitcast(I32), 0)
        for g in range(4):
            nc.sync.dma_start(k_scales[32 * g:32 * g + 4, :].bitcast(I32),
                              keys_scales[0, 4 * g:4 * g + 4, :].bitcast(I32))
        nc.sync.dma_start(k_words[:].bitcast(I32), keys_words[0].bitcast(I32))
        nc.sync.dma_start(n_words[:].bitcast(I32),
                          notes_words[0].rearrange("p n t -> p (n t)").bitcast(I32))
        for g in range(4):
            nc.sync.dma_start(n_scales[32 * g:32 * g + 4, :].bitcast(I32),
                              notes_scales[0, 4 * g:4 * g + 4, :].bitcast(I32))
        sources = [offs, offs2, offs3, offs4, offs5, offs6]
        for j in (0, 2, 1, 3, 4, 5):
            nc.sync.dma_start(lists[j][:], sources[j])
        nc.vector.memset(f1[:], 0.0)

        for u in range(2):
            rows = slice(u * Q // 2, (u + 1) * Q // 2)
            nc.vector.tensor_copy(q_bf[:, rows, :], q_raw[:, :, rows].rearrange("p j q -> p q j"))
        for u in range(2):
            rows = slice(u * Q // 2, (u + 1) * Q // 2)
            nc.vector.quantize_mx(out=q_codes[:, rows].bitcast(FP8X4), scales=q_scales[:, rows],
                                  in_=q_bf[:, rows, :].rearrange("p q j -> p (q j)"))

        def scores(name, c, words, scales):
            bank = ps.tile([P, N_PASS], F32, name=name)
            nc.tensor.matmul_mx(out=bank[:], lhsT=q_codes[:].bitcast(FP8X4), lhsT_scale=q_scales[:],
                                rhs=words, rhs_scale=scales[:, c * N_PASS:(c + 1) * N_PASS],
                                start=True, stop=True)
            return bank

        a_banks = []
        for c in range(T // N_PASS):
            cols = slice(c * N_PASS, (c + 1) * N_PASS)
            bank = scores("a%d" % c, c, k_words[:, 2 * c * N_PASS:2 * (c + 1) * N_PASS].bitcast(FP4X4), k_scales)
            a_banks.append(bank)
            if c % 2 == 0:
                nc.scalar.activation(a[:, cols], bank[:], COPY)
            else:
                nc.vector.tensor_copy(a[:, cols], bank[:])
        for c in range(U // N_PASS):
            cols = slice(c * N_PASS, (c + 1) * N_PASS)
            bank = scores("b%d" % c, c, n_words[:, cols].bitcast(FP8X4), n_scales)
            nc.scalar.activation(b[:, cols], bank[:], COPY)

        def picked(window, j, h):
            return window[:].indirect(lists[j][:, h * HALF_COLS:(h + 1) * HALF_COLS])

        for h in range(2):
            tok1 = sb.tile([P, HALF], F32, name="tok1")
            note1 = sb.tile([P, HALF], F32, name="note1_%d" % h)
            tok2 = sb.tile([P, HALF], F32, name="tok2")
            neg_note2 = sb.tile([P, HALF], F32, name="neg_note2_%d" % h)
            w = sb.tile([P, HALF], F32, name="w")
            neg_v = sb.tile([P, HALF], F32, name="neg_v")
            if h == 0:
                nc.vector.tensor_copy(tok1[:], picked(a, 0, h))
                nc.vector.tensor_copy(tok2[:], picked(a, 2, h))
                nc.scalar.activation(neg_note2[:], picked(b, 3, h), COPY, scale=-1.0)
                nc.vector.tensor_copy(note1[:], picked(b, 1, h))
                nc.vector.scalar_tensor_tensor(neg_v[:], tok2[:], -1.0, neg_note2[:], ALU.mult, ALU.min)
                nc.vector.tensor_tensor(w[:], tok1[:], note1[:], ALU.max)
            else:
                nc.scalar.activation(neg_note2[:], picked(b, 3, h), COPY, scale=-1.0)
                nc.scalar.activation(note1[:], picked(b, 1, h), COPY)
                nc.scalar.activation(tok2[:], picked(a, 2, h), COPY)
                nc.scalar.activation(tok1[:], picked(a, 0, h), COPY)
                nc.vector.scalar_tensor_tensor(neg_v[:], tok2[:], -1.0, neg_note2[:], ALU.mult, ALU.min)
                nc.vector.tensor_tensor(w[:], tok1[:], note1[:], ALU.max)
            nc.vector.tensor_tensor(picked(f1, 4, h), w[:], neg_v[:], ALU.add)

        last = slice(T - N_PASS, T)
        nc.gpsimd.tensor_tensor(cc[:, last], a[:, last], f1[:, last], ALU.subtract)
        for c in range(T // N_PASS - 1):
            cols = slice(c * N_PASS, (c + 1) * N_PASS)
            nc.vector.tensor_tensor(cc[:, cols], a_banks[c][:], f1[:, cols], ALU.subtract)
        y0 = sb.tile([P, HALF], F32)
        y1 = sb.tile([P, HALF], F32)
        nc.vector.tensor_copy(y0[:], picked(cc, 5, 0))
        nc.scalar.activation(y1[:], picked(cc, 5, 1), COPY)
        nc.sync.dma_start(out[:, 0:HALF], y0[:])
        nc.scalar.dma_start(out[:, HALF:SLOTS], y1[:])
